import numpy as np
import ml_dtypes

BF16 = ml_dtypes.bfloat16


def bf(x):
    return np.asarray(x, np.float32).astype(BF16)


def f32(x):
    return np.asarray(x, np.float32)


def f64(x):
    return np.asarray(x).astype(np.float64)


def striped(idx):
    return np.tile(idx.reshape(-1, 16).T, (8, 1))


def rows(idx, k):
    return np.tile(idx, (k, 1))


def look(tab, idx):
    return np.take_along_axis(f64(tab), rows(idx, len(tab)), axis=1)


K, S, D, V, N = 256, 2048, 4, 512, 2048


def setup_inputs():
    return {"tab": f32(np.random.standard_normal((K, S))), "x0": f32(np.random.standard_normal((K, V))), "offs": striped(np.random.permutation(S)[:N])}


def reference(tab, x0, offs):
    idx = offs[:16].T.reshape(-1)
    x = f64(x0)
    for d in range(D):
        x = np.maximum(x, look(tab, idx[d * V:(d + 1) * V]))
    return x

@@ -1,0 +1,39 @@
+import concourse.mybir as mybir
+
+P = 128
+ROWS = 256
+COLUMNS = 2048
+WIDTH = 512
+NEIGHBOURS = 4
+STRIPE = 16
+F32, U16 = mybir.dt.float32, mybir.dt.uint16
+MAX = mybir.AluOpType.max
+
+BYTES = 4 * (ROWS * COLUMNS + 2 * ROWS * WIDTH) + 2 * P * (NEIGHBOURS * WIDTH // STRIPE)
+
+
+def tile_lookup_pool_max_out_kernel(tc, tab, x0, offs, out):
+    nc = tc.nc
+    with tc.tile_pool(name="held", bufs=1) as held:
+        offsets = held.tile([P, NEIGHBOURS * WIDTH // STRIPE], U16, name="offsets")
+        nc.sync.dma_start(offsets[:], offs)
+
+        windows, centres = [], []
+        for b in range(ROWS // P):
+            rows = slice(b * P, (b + 1) * P)
+            window = held.tile([P, COLUMNS], F32, name=f"window{b}")
+            nc.sync.dma_start(window[:], tab[rows, :])
+            windows.append(window)
+            centre = held.tile([P, WIDTH], F32, name=f"centre{b}")
+            nc.sync.dma_start(centre[:], x0[rows, :])
+            centres.append(centre)
+
+        per_list = WIDTH // STRIPE
+        for b in range(ROWS // P):
+            largest = centres[b]
+            for d in range(NEIGHBOURS):
+                neighbours = offsets[:, d * per_list : (d + 1) * per_list]
+                larger = held.tile([P, WIDTH], F32, name=f"larger{b}_{d}")
+                nc.vector.tensor_tensor(larger[:], windows[b][:].indirect(neighbours), largest[:], MAX)
+                largest = larger
+            nc.sync.dma_start(out[b * P : (b + 1) * P, :], largest[:])

@@ -28,12 +28,15 @@ def tile_lookup_pool_max_out_kernel(tc, tab, x0, offs, out):
             nc.sync.dma_start(centre[:], x0[rows, :])
             centres.append(centre)
 
-        per_list = WIDTH // STRIPE
+        half = WIDTH // 2
         for b in range(ROWS // P):
-            largest = centres[b]
+            largest = [centres[b][:, h * half : (h + 1) * half] for h in range(2)]
             for d in range(NEIGHBOURS):
-                neighbours = offsets[:, d * per_list : (d + 1) * per_list]
-                larger = held.tile([P, WIDTH], F32, name=f"larger{b}_{d}")
-                nc.vector.tensor_tensor(larger[:], windows[b][:].indirect(neighbours), largest[:], MAX)
-                largest = larger
-            nc.sync.dma_start(out[b * P : (b + 1) * P, :], largest[:])
+                for h in range(2):
+                    first = (d * WIDTH + h * half) // STRIPE
+                    neighbours = offsets[:, first : first + half // STRIPE]
+                    larger = held.tile([P, half], F32, name=f"larger{b}_{d}_{h}")
+                    nc.vector.tensor_tensor(larger[:], windows[b][:].indirect(neighbours), largest[h], MAX)
+                    largest[h] = larger[:]
+            for h in range(2):
+                nc.sync.dma_start(out[b * P : (b + 1) * P, h * half : (h + 1) * half], largest[h])

import concourse.mybir as mybir

P = 128
ROWS = 256
COLUMNS = 2048
WIDTH = 512
NEIGHBOURS = 4
STRIPE = 16
F32, U16 = mybir.dt.float32, mybir.dt.uint16
MAX = mybir.AluOpType.max

BYTES = 4 * (ROWS * COLUMNS + 2 * ROWS * WIDTH) + 2 * P * (NEIGHBOURS * WIDTH // STRIPE)


def tile_lookup_pool_max_out_kernel(tc, tab, x0, offs, out):
    nc = tc.nc
    with tc.tile_pool(name="held", bufs=1) as held:
        offsets = held.tile([P, NEIGHBOURS * WIDTH // STRIPE], U16, name="offsets")
        nc.sync.dma_start(offsets[:], offs)

        windows, centres = [], []
        for b in range(ROWS // P):
            rows = slice(b * P, (b + 1) * P)
            window = held.tile([P, COLUMNS], F32, name=f"window{b}")
            nc.sync.dma_start(window[:], tab[rows, :])
            windows.append(window)
            centre = held.tile([P, WIDTH], F32, name=f"centre{b}")
            nc.sync.dma_start(centre[:], x0[rows, :])
            centres.append(centre)

        half = WIDTH // 2
        for b in range(ROWS // P):
            largest = [centres[b][:, h * half : (h + 1) * half] for h in range(2)]
            for d in range(NEIGHBOURS):
                for h in range(2):
                    first = (d * WIDTH + h * half) // STRIPE
                    neighbours = offsets[:, first : first + half // STRIPE]
                    larger = held.tile([P, half], F32, name=f"larger{b}_{d}_{h}")
                    nc.vector.tensor_tensor(larger[:], windows[b][:].indirect(neighbours), largest[h], MAX)
                    largest[h] = larger[:]
            for h in range(2):
                nc.sync.dma_start(out[b * P : (b + 1) * P, h * half : (h + 1) * half], largest[h])
